import numpy as np
import ml_dtypes


def mxq(x, axis, fmt="e4m3"):
    dtype, down = {"e4m3": (ml_dtypes.float8_e4m3fn, 7), "e5m2": (ml_dtypes.float8_e5m2, 14)}[fmt]
    v = np.moveaxis(np.asarray(x, np.float32).astype(ml_dtypes.bfloat16).astype(np.float64), axis, -1)
    blocks = v.reshape(v.shape[:-1] + (-1, 32))
    amax = np.abs(blocks).max(-1, keepdims=True)
    byte = np.maximum(np.where(amax > 0, np.frexp(amax)[1] - 1 + 127, 0) - down, 1)
    scale = np.exp2(byte - 127.0)
    codes = (blocks / scale).astype(np.float32).astype(dtype).astype(np.float64)
    return np.moveaxis((codes * scale).reshape(v.shape), -1, axis)


WIDE = False


def mx_kscale(k):
    if not WIDE:
        return np.ones(k)
    levels = np.array([10, -10, 5, -5, 0])
    if k % 512:
        return np.exp2(np.random.permutation(np.resize(levels, k // 32))).repeat(32)
    a = np.empty((k // 512, 16))
    for p in range(k // 512):
        a[p, :8] = np.random.permutation(np.resize(levels, 8))
        for g in range(8):
            far = levels[np.abs(levels - a[p, g]) >= 10]
            a[p, g + 8] = far[np.random.randint(len(far))]
    return np.exp2(a.ravel()).repeat(32)


def f64(x):
    return np.asarray(x).astype(np.float64)


def striped(idx):
    return np.tile(idx.reshape(-1, 16).T, (8, 1)).astype(np.uint16)


def unstriped(offs):
    return offs[:16].T.reshape(-1).astype(np.int64)


E2M1 = np.array([0.0, 0.5, 1.0, 1.5, 2.0, 3.0, 4.0, 6.0, -0.0, -0.5, -1.0, -1.5, -2.0, -3.0, -4.0, -6.0])


def pack_weight(w, fmt):
    k, n = w.shape
    w = f64(np.asarray(w, np.float32).astype(ml_dtypes.bfloat16)).reshape(k // 32, 32, n)
    amax = np.abs(w).max(1)
    if fmt == "e4m3":
        byte = np.frexp(amax)[1] - 1 + 127 - 7
    else:
        mant, ex = np.frexp(amax / 6.0)
        byte = np.where(mant > 0.5, ex, ex - 1) + 127
    byte = np.clip(np.where(amax > 0, byte, 1), 1, 254)
    scaled = (w * np.exp2(127.0 - byte)[:, None, :]).reshape(k, n).astype(np.float32)
    by_word = np.ascontiguousarray(scaled.reshape(k // 512, 128, 4, n).transpose(0, 1, 3, 2))
    if fmt == "e4m3":
        words = by_word.astype(ml_dtypes.float8_e4m3fn).view(np.uint8)
    else:
        c = by_word.astype(ml_dtypes.float4_e2m1fn).view(np.uint8) & 0xF
        words = (c[..., 0::2] | (c[..., 1::2] << 4)).reshape(k // 512, 128, 2 * n)
    return np.ascontiguousarray(words), np.ascontiguousarray(byte.astype(np.uint8).reshape(k // 512, 16, n))


def unpack_weight(words, scales, fmt):
    g, _, n = scales.shape
    words = np.ascontiguousarray(words).reshape(g, 128, n, -1)
    if fmt == "e4m3":
        vals = words.view(ml_dtypes.float8_e4m3fn).astype(np.float64)
    else:
        nib = np.empty((g, 128, n, 4), np.uint8)
        nib[..., 0::2] = words & 0xF
        nib[..., 1::2] = words >> 4
        vals = E2M1[nib]
    vals = vals * np.repeat(np.exp2(scales.astype(np.float64) - 127.0), 8, axis=1)[..., None]
    return vals.transpose(0, 1, 3, 2).reshape(g * 512, n)


def gelu(v):
    return 0.5 * v * (1.0 + np.tanh(np.sqrt(2.0 / np.pi) * (v + 0.044715 * v**3)))


K, H, T, S, T2, P = 1536, 1024, 4096, 1024, 2048, 512


def setup_inputs():
    n = np.random.standard_normal
    uni = np.random.uniform
    s = mx_kscale(K)[:, None]
    u = mx_kscale(H)[:, None]
    d = {}
    d["tab_words"], d["tab_scales"] = pack_weight(n((K, T)) * s, "e4m3")
    d["offs"] = striped(np.random.permutation(T)[:S])
    d["offs2"] = striped(np.random.permutation(T2)[:S])
    d["offs3"] = striped(np.random.permutation(T2)[:P])
    d["offs4"] = striped(np.random.permutation(T2)[:P])
    d["w1"] = (n((K, H)) / K ** 0.5 / s).astype(np.float32)
    d["gain"] = (uni(0.26, 0.42, H) * np.sign(n(H)) * u[:, 0]).astype(np.float32)
    d["wgs"] = np.exp(0.3 * np.clip(n((128, S)), -1.5, 1.5)).astype(np.float32)
    d["page0"] = (uni(-2.5, 2.5, (H, T2)) * u).astype(np.float32)
    d["reread"] = (uni(0.6, 1.0, H) / u[:, 0]).astype(np.float32)
    d["swing"] = (uni(1.0, 2.0, H) * u[:, 0]).astype(np.float32)
    d["w4_words"], d["w4_scales"] = pack_weight(n((H, H)) / H ** 0.5 / u, "e2m1")
    d["mirror"] = (uni(0.5, 1.1, H) / u[:, 0]).astype(np.float32)
    return d


def reference(tab_words, tab_scales, offs, offs2, offs3, offs4, w1, gain, wgs, page0,
              reread, swing, w4_words, w4_scales, mirror):
    v = unpack_weight(tab_words, tab_scales, "e4m3")[:, unstriped(offs)]
    h = f64(gain)[:, None] * np.abs(mxq(f64(w1), 0, "e4m3").T @ v)
    page = f64(page0).copy()
    page[:, unstriped(offs2)] = np.tile(f64(wgs), (H // 128, 1)) * h
    x = f64(swing)[:, None] * np.sin(f64(reread)[:, None] * page[:, unstriped(offs3)])
    w4 = unpack_weight(w4_words, w4_scales, "e2m1")
    y = w4.T @ mxq(x, 0, "e4m3")
    b = f64(mirror)[:, None] * page[:, unstriped(offs4)]
    return np.sqrt(np.square(y) + np.square(b))

@@ -1,0 +1,343 @@
+from contextlib import ExitStack
+
+import concourse.mybir as mybir
+from concourse.masks import make_identity
+
+F32 = mybir.dt.float32
+BF16 = mybir.dt.bfloat16
+I32 = mybir.dt.int32
+U32 = mybir.dt.uint32
+U16 = mybir.dt.uint16
+U8 = mybir.dt.uint8
+FP8X4 = mybir.dt.float8_e4m3fn_x4
+FP4X4 = mybir.dt.float4_e2m1fn_x4
+ACT = mybir.ActivationFunctionType
+MULT = mybir.AluOpType.mult
+ADD = mybir.AluOpType.add
+
+K, H, T, S, T2, M = 1536, 1024, 4096, 1024, 2048, 512
+FLOPS = 2 * K * H * S + 2 * H * H * M
+
+P = 128
+BANK = 512
+K_PASSES = K // 512
+R_PASSES = H // 512
+TILES = H // P
+HALVES = S // BANK
+W1_LOADS = ((0, 1), (1, 2), (2, 3), (3, 4), (4, 6), (6, 8))
+EARLY_MIRROR = 5
+SQUARE_ON = "SSSSVVVV"
+OWN_PAGES = 5
+
+
+def tile_list_pressure_tap_survey_kernel(
+    tc, tab_words, tab_scales, offs, offs2, offs3, offs4, w1, gain, wgs, page0,
+    reread, swing, w4_words, w4_scales, mirror, out,
+):
+    nc = tc.nc
+    with ExitStack() as ctx:
+        lists = ctx.enter_context(tc.tile_pool(name="lists", bufs=1))
+        sb = ctx.enter_context(tc.tile_pool(name="sb", bufs=1))
+        psum = ctx.enter_context(tc.psum_pool(name="psum", bufs=1))
+
+        def sbuf(shape, dtype, name, tag=None):
+            return sb.tile(shape, dtype, name=name, tag=tag or name, align_bytes=64)
+
+        idx = lists.tile([P, S // 16], U16, name="idx")
+        idx2 = lists.tile([P, S // 16], U16, name="idx2")
+        idx3 = lists.tile([P, M // 16], U16, name="idx3")
+        idx4 = lists.tile([P, M // 16], U16, name="idx4")
+
+        tab_sc = sbuf([P, T], U8, "tab_sc")
+        nc.vector.memset(tab_sc[:].bitcast(I32), 0)
+        ident_f = sbuf([P, P], F32, "ident_f")
+        make_identity(nc, ident_f[:])
+        for q in range(4):
+            nc.gpsimd.dma_start(
+                out=tab_sc[32 * q : 32 * q + 4 * K_PASSES, :].bitcast(I32),
+                in_=tab_scales[:, 4 * q : 4 * q + 4, :].bitcast(I32),
+            )
+        vec_rows = sbuf([P, P], F32, "vec_rows")
+        nc.vector.memset(vec_rows[32:64, :], 0.0)
+        nc.vector.memset(vec_rows[64:128, :], 0.0)
+        ident_b = sbuf([P, P], BF16, "ident_b")
+        nc.vector.tensor_copy(ident_b[:], ident_f[:])
+        w4_sc = sbuf([P, R_PASSES, H], U8, "w4_sc")
+        nc.vector.memset(w4_sc[:].rearrange("p a n -> p (a n)").bitcast(I32), 0)
+
+        warm = sbuf([P, 1], F32, "warm")
+        nc.vector.memset(warm[:], 1.0)
+        warm_sin = sbuf([P, 1], F32, "warm_sin")
+        nc.scalar.activation(warm_sin[:], warm[:], ACT.Sin)
+
+        def load_table(a):
+            words = sbuf([P, T], I32, "tab%d" % a)
+            nc.sync.dma_start(
+                out=words[:], in_=tab_words[a].rearrange("p n i -> p (n i)").bitcast(I32)
+            )
+            return words
+
+        raws = {}
+
+        def load_w1(first, last):
+            for a in range(K_PASSES):
+                tag = "chain" if (first, a) == (2, K_PASSES - 1) else "raw%d_%d" % (first, a)
+                raw = sbuf([P, 4, P * (last - first)], F32, "raw", tag=tag)
+                nc.sync.dma_start(
+                    out=raw[:],
+                    in_=w1[512 * a : 512 * (a + 1), P * first : P * last].rearrange(
+                        "(p i) c -> p i c", i=4
+                    ),
+                )
+                for c in range(first, last):
+                    raws[c, a] = raw[:, :, P * (c - first) : P * (c - first + 1)]
+
+        pages = {}
+
+        def load_page(c):
+            tag = "page%d" % c if c < OWN_PAGES else "tab%d" % (c - OWN_PAGES)
+            pages[c] = sbuf([P, T2], F32, "page", tag=tag)
+            nc.sync.dma_start(out=pages[c][:], in_=page0[P * c : P * (c + 1), :])
+
+        nc.sync.dma_start(idx[:], offs)
+        tabs = [load_table(0)]
+        load_w1(*W1_LOADS[0])
+        for v, vec in enumerate((gain, reread, swing, mirror)):
+            nc.sync.dma_start(
+                out=vec_rows[TILES * v : TILES * (v + 1), :],
+                in_=vec.rearrange("(c p) -> c p", p=P),
+            )
+        tabs.append(load_table(1))
+        tabs.append(load_table(2))
+        nc.sync.dma_start(idx2[:], offs2)
+        wgs_sb = sbuf([P, S], F32, "wgs_sb")
+        nc.sync.dma_start(out=wgs_sb[:, 0:BANK], in_=wgs[:, 0:BANK])
+        load_page(0)
+        load_w1(*W1_LOADS[1])
+        nc.sync.dma_start(out=wgs_sb[:, BANK:S], in_=wgs[:, BANK:S])
+        nc.sync.dma_start(idx3[:], offs3)
+        for n, (first, last) in enumerate(W1_LOADS[2:]):
+            load_w1(first, last)
+            load_page(n + 1)
+        nc.sync.dma_start(idx4[:], offs4)
+        w4 = sbuf([P, R_PASSES, 2 * H], U8, "w4")
+        nc.sync.dma_start(
+            out=w4[:].bitcast(I32), in_=w4_words.rearrange("a p n -> p a n").bitcast(I32)
+        )
+        for q in range(4):
+            nc.sync.dma_start(
+                out=w4_sc[32 * q : 32 * q + 4, :, :].bitcast(I32),
+                in_=w4_scales[:, 4 * q : 4 * q + 4, :].rearrange("a r n -> r a n").bitcast(I32),
+            )
+
+        vec_t = psum.tile([P, P], F32, name="vec_t", tag="t1", bufs=1)
+        nc.tensor.transpose(vec_t[:], vec_rows[:], ident_f[:])
+        vecs = sbuf([P, 3 * TILES], F32, "vecs")
+        nc.scalar.copy(vecs[:], vec_t[:, 0 : 3 * TILES])
+        mirror_sq = sbuf([P, TILES], F32, "mirror_sq")
+        nc.scalar.activation(mirror_sq[:], vec_t[:, 3 * TILES : 4 * TILES], ACT.Square)
+
+        def column(v, c):
+            return vecs[:, TILES * v + c : TILES * v + c + 1]
+
+        grouped = {}
+
+        def round_w1(c):
+            for a in range(K_PASSES):
+                g = sbuf([P, P, 4], BF16, "w1_grouped", tag="w1g%d_%d" % (a, c % 2))
+                nc.scalar.copy(
+                    g[:].rearrange("p (c j) i -> p c i j", j=4),
+                    raws[c, a].rearrange("p i (c j) -> p c i j", j=4),
+                )
+                grouped[c, a] = g
+
+        w1q = {}
+
+        def quantise_w1(c, tag):
+            codes = sbuf([P, K_PASSES, P], U32, "w1_codes", tag=tag)
+            scales = sbuf([P, K_PASSES, P], U8, "w1_scales%d" % c)
+            for a in range(K_PASSES):
+                nc.vector.quantize_mx(
+                    out=codes[:, a, :].bitcast(FP8X4),
+                    scales=scales[:, a, :],
+                    in_=grouped[c, a][:].rearrange("p c i -> p (c i)"),
+                )
+            w1q[c] = (codes, scales)
+
+        round_w1(0)
+        quantise_w1(0, "w1_codes0")
+
+        picked = {}
+        picked_sc = sbuf([P, S], U8, "picked_sc")
+        for a in range(K_PASSES):
+            for h in range(HALVES):
+                pk = sbuf([P, BANK], U32, "picked%d_%d" % (a, h))
+                nc.vector.tensor_copy(
+                    pk[:], tabs[a][:].bitcast(U32).indirect(idx[:, 32 * h : 32 * (h + 1)])
+                )
+                picked[a, h] = pk
+            if a == 0:
+                nc.vector.tensor_copy(picked_sc[:], tab_sc[:].indirect(idx[:]))
+            load_page(OWN_PAGES + a)
+
+        def first_product(c, h):
+            codes, scales = w1q[c]
+            acc = psum.tile([P, BANK], F32, name="acc", tag="acc", bufs=2)
+            for a in range(K_PASSES):
+                nc.tensor.matmul_mx(
+                    out=acc[:],
+                    lhsT=codes[:, a, :].bitcast(FP8X4),
+                    lhsT_scale=scales[:, a, :],
+                    rhs=picked[a, h][:].bitcast(FP8X4),
+                    rhs_scale=picked_sc[4 * a : P, BANK * h : BANK * (h + 1)],
+                    start=(a == 0),
+                    stop=(a == K_PASSES - 1),
+                )
+            return acc
+
+        h_tiles = {}
+
+        def make_h(c):
+            magnitude = sbuf([P, S], F32, "magnitude", tag="chain")
+            h_tiles[c] = sbuf([P, S], F32, "h_tile", tag="h%d" % (c % 3))
+            for h in range(HALVES):
+                js = slice(BANK * h, BANK * (h + 1))
+                nc.scalar.activation(magnitude[:, js], first_product(c, h)[:], ACT.Abs)
+                nc.scalar.activation(
+                    h_tiles[c][:, js], magnitude[:, js], ACT.Copy, scale=column(0, c)
+                )
+
+        x_t = {}
+
+        def make_x(c):
+            taps = sbuf([P, M], F32, "taps", tag="w1g%d_%d" % (K_PASSES - 1, c % 2))
+            nc.vector.tensor_copy(taps[:], pages[c][:].indirect(idx3[:]))
+            sine = sbuf([P, M], F32, "sine", tag="chain")
+            nc.scalar.activation(sine[:], taps[:], ACT.Sin, scale=column(1, c))
+            x_rows = sbuf([P, M], BF16, "x_rows")
+            nc.scalar.activation(x_rows[:], sine[:], ACT.Copy, scale=column(2, c))
+            turned = psum.tile([P, 4, P], BF16, name="turned", tag="t1", bufs=1)
+            for mb in range(4):
+                nc.tensor.transpose(turned[:, mb, :], x_rows[:, P * mb : P * (mb + 1)], ident_b[:])
+            b, cc = divmod(c, 4)
+            if cc == 0:
+                x_t[b] = sbuf([P, 4, 2, P], F32, "x_t", tag="x_t")
+            nc.scalar.copy(
+                x_t[b][:, :, :, 32 * cc : 32 * (cc + 1)],
+                turned[:].bitcast(F32).rearrange("m b (p u) -> m b u p", u=2),
+            )
+
+        x_grouped = {}
+
+        def deal_x(b):
+            xg = sbuf([P, M, 2], F32, "x_grouped", tag="x_grouped")
+            for hb in range(2):
+                back = psum.tile([P, 2, 2, P], F32, name="back", tag="t2", bufs=2)
+                for mb in range(2):
+                    for u in range(2):
+                        nc.tensor.transpose(
+                            back[:, mb, u, :], x_t[b][:, 2 * hb + mb, u, :], ident_f[:]
+                        )
+                nc.scalar.copy(
+                    xg[:, 256 * hb : 256 * (hb + 1), :].rearrange("p (b m) u -> p b m u", b=2),
+                    back[:].rearrange("p b u m -> p b m u"),
+                )
+            x_grouped[b] = xg
+
+        xq = {}
+
+        def quantise_x(b, tag):
+            codes = sbuf([P, M], U32, "x_codes", tag=tag)
+            scales = sbuf([P, M], U8, "x_scales%d" % b)
+            nc.vector.quantize_mx(
+                out=codes[:].bitcast(FP8X4),
+                scales=scales[:],
+                in_=x_grouped[b][:].rearrange("p m u -> p (m u)").bitcast(BF16),
+            )
+            xq[b] = (codes, scales)
+
+        h_tiles[0] = sbuf([P, S], F32, "h_tile", tag="h0")
+        for h in range(HALVES):
+            js = slice(BANK * h, BANK * (h + 1))
+            if h == 1:
+                round_w1(1)
+                quantise_w1(1, "w1_codes1")
+            gained = sbuf([P, BANK], F32, "gained", tag="raw%d_%d" % (h, K_PASSES - 1))
+            nc.scalar.activation(gained[:], wgs_sb[:, js], ACT.Copy, scale=column(0, 0))
+            nc.scalar.activation(h_tiles[0][:, js], first_product(0, h)[:], ACT.Abs)
+            nc.vector.tensor_tensor(
+                pages[0][:].indirect(idx2[:, 32 * h : 32 * (h + 1)]),
+                h_tiles[0][:, js], gained[:], MULT,
+            )
+
+        for c in range(TILES):
+            if c + 2 < TILES:
+                round_w1(c + 2)
+            if c + 1 < TILES:
+                make_h(c + 1)
+            if c == 4:
+                deal_x(0)
+            if c > 0:
+                nc.vector.tensor_tensor(
+                    pages[c][:].indirect(idx2[:]), h_tiles[c][:], wgs_sb[:], MULT
+                )
+            if c + 2 < TILES:
+                quantise_w1(c + 2, "h%d" % (c % 3))
+            if c == 6:
+                quantise_x(0, "h%d" % (c % 3))
+            make_x(c)
+
+        deal_x(1)
+        quantise_x(1, "x_codes1")
+
+        early = sbuf([P, EARLY_MIRROR, M], F32, "early", tag="h%d" % ((TILES - 1) % 3))
+        late = sbuf([P, TILES - EARLY_MIRROR, M], F32, "late", tag="x_grouped")
+        held = sbuf([P, 2, M], F32, "held", tag="x_t")
+        nc.scalar.activation(held[:, 0, 0:1], warm[:], ACT.Sqrt)
+
+        totals = []
+        for c in range(TILES):
+            taps4 = early[:, c, :] if c < EARLY_MIRROR else late[:, c - EARLY_MIRROR, :]
+            nc.vector.tensor_copy(taps4, pages[c][:].indirect(idx4[:]))
+            if c < 2:
+                total = sbuf([P, M], F32, "total", tag=("chain", "x_rows")[c])[:]
+            elif c < 4:
+                total = held[:, c - 2, :]
+            else:
+                total = sbuf([P, M], F32, "total%d" % c)[:]
+            if SQUARE_ON[c] == "S":
+                nc.scalar.activation(total, taps4, ACT.Square)
+            elif SQUARE_ON[c] == "V":
+                nc.vector.tensor_tensor(total, taps4, taps4, MULT)
+            else:
+                nc.gpsimd.tensor_tensor(total, taps4, taps4, MULT)
+            totals.append(total)
+
+        y_tags = [("y", 3)] * 3 + [("acc", 2)] * 2 + [("t2", 2)] * 2 + [("t1", 1)]
+        ys = []
+        for c in range(TILES):
+            tag, bufs = y_tags[c]
+            ys.append(psum.tile([P, M], F32, name="y", tag=tag, bufs=bufs))
+        for b in range(R_PASSES):
+            codes, scales = xq[b]
+            for c in range(TILES):
+                nc.tensor.matmul_mx(
+                    out=ys[c][:],
+                    lhsT=w4[:, b, 2 * P * c : 2 * P * (c + 1)].bitcast(FP4X4),
+                    lhsT_scale=w4_sc[:, b, P * c : P * (c + 1)],
+                    rhs=codes[:].bitcast(FP8X4),
+                    rhs_scale=scales[:],
+                    start=(b == 0),
+                    stop=(b == R_PASSES - 1),
+                )
+        y_sq = []
+        for c in range(TILES):
+            sq = sbuf([P, M], F32, "y_sq", tag="raw%d_%d" % ((3, 4, 6)[c // 3], c % 3))
+            nc.scalar.activation(sq[:], ys[c][:], ACT.Square)
+            y_sq.append(sq)
+        for c in range(TILES):
+            nc.vector.scalar_tensor_tensor(
+                totals[c], totals[c], mirror_sq[:, c : c + 1], y_sq[c][:], MULT, ADD
+            )
+            nc.scalar.activation(totals[c], totals[c], ACT.Sqrt)
+            nc.sync.dma_start(out=out[P * c : P * (c + 1), :], in_=totals[c])

@@ -26,7 +26,7 @@ TILES = H // P
 HALVES = S // BANK
 W1_LOADS = ((0, 1), (1, 2), (2, 3), (3, 4), (4, 6), (6, 8))
 EARLY_MIRROR = 5
-SQUARE_ON = "SSSSVVVV"
+SQUARE_ON = "SSSSSVVV"
 OWN_PAGES = 5
 
 
@@ -52,11 +52,6 @@ def tile_list_pressure_tap_survey_kernel(
         nc.vector.memset(tab_sc[:].bitcast(I32), 0)
         ident_f = sbuf([P, P], F32, "ident_f")
         make_identity(nc, ident_f[:])
-        for q in range(4):
-            nc.gpsimd.dma_start(
-                out=tab_sc[32 * q : 32 * q + 4 * K_PASSES, :].bitcast(I32),
-                in_=tab_scales[:, 4 * q : 4 * q + 4, :].bitcast(I32),
-            )
         vec_rows = sbuf([P, P], F32, "vec_rows")
         nc.vector.memset(vec_rows[32:64, :], 0.0)
         nc.vector.memset(vec_rows[64:128, :], 0.0)
@@ -100,16 +95,21 @@ def tile_list_pressure_tap_survey_kernel(
             nc.sync.dma_start(out=pages[c][:], in_=page0[P * c : P * (c + 1), :])
 
         nc.sync.dma_start(idx[:], offs)
+        nc.sync.dma_start(idx2[:], offs2)
         tabs = [load_table(0)]
+        for q in range(4):
+            nc.sync.dma_start(
+                out=tab_sc[32 * q : 32 * q + 4 * K_PASSES, :].bitcast(I32),
+                in_=tab_scales[:, 4 * q : 4 * q + 4, :].bitcast(I32),
+            )
+        tabs.append(load_table(1))
         load_w1(*W1_LOADS[0])
         for v, vec in enumerate((gain, reread, swing, mirror)):
             nc.sync.dma_start(
                 out=vec_rows[TILES * v : TILES * (v + 1), :],
                 in_=vec.rearrange("(c p) -> c p", p=P),
             )
-        tabs.append(load_table(1))
         tabs.append(load_table(2))
-        nc.sync.dma_start(idx2[:], offs2)
         wgs_sb = sbuf([P, S], F32, "wgs_sb")
         nc.sync.dma_start(out=wgs_sb[:, 0:BANK], in_=wgs[:, 0:BANK])
         load_page(0)
@@ -156,7 +156,7 @@ def tile_list_pressure_tap_survey_kernel(
         def quantise_w1(c, tag):
             codes = sbuf([P, K_PASSES, P], U32, "w1_codes", tag=tag)
             scales = sbuf([P, K_PASSES, P], U8, "w1_scales%d" % c)
-            for a in range(K_PASSES):
+            for a in ((0, 1, 2) if c < 2 else (2, 0, 1)):
                 nc.vector.quantize_mx(
                     out=codes[:, a, :].bitcast(FP8X4),
                     scales=scales[:, a, :],
@@ -212,9 +212,9 @@ def tile_list_pressure_tap_survey_kernel(
         def make_x(c):
             taps = sbuf([P, M], F32, "taps", tag="w1g%d_%d" % (K_PASSES - 1, c % 2))
             nc.vector.tensor_copy(taps[:], pages[c][:].indirect(idx3[:]))
-            sine = sbuf([P, M], F32, "sine", tag="chain")
+            sine = sbuf([P, M], F32, "sine", tag="chain" if c < 7 else "x_rows")
             nc.scalar.activation(sine[:], taps[:], ACT.Sin, scale=column(1, c))
-            x_rows = sbuf([P, M], BF16, "x_rows")
+            x_rows = sbuf([P, M], BF16, "x_rows", tag="x_rows" if c < 7 else "chain")
             nc.scalar.activation(x_rows[:], sine[:], ACT.Copy, scale=column(2, c))
             turned = psum.tile([P, 4, P], BF16, name="turned", tag="t1", bufs=1)
             for mb in range(4):
@@ -292,7 +292,7 @@ def tile_list_pressure_tap_survey_kernel(
 
         early = sbuf([P, EARLY_MIRROR, M], F32, "early", tag="h%d" % ((TILES - 1) % 3))
         late = sbuf([P, TILES - EARLY_MIRROR, M], F32, "late", tag="x_grouped")
-        held = sbuf([P, 2, M], F32, "held", tag="x_t")
+        held = sbuf([P, EARLY_MIRROR - 2, M], F32, "held", tag="x_t")
         nc.scalar.activation(held[:, 0, 0:1], warm[:], ACT.Sqrt)
 
         totals = []
@@ -300,8 +300,8 @@ def tile_list_pressure_tap_survey_kernel(
             taps4 = early[:, c, :] if c < EARLY_MIRROR else late[:, c - EARLY_MIRROR, :]
             nc.vector.tensor_copy(taps4, pages[c][:].indirect(idx4[:]))
             if c < 2:
-                total = sbuf([P, M], F32, "total", tag=("chain", "x_rows")[c])[:]
-            elif c < 4:
+                total = sbuf([P, M], F32, "total", tag=("x_rows", "chain")[c])[:]
+            elif c < EARLY_MIRROR:
                 total = held[:, c - 2, :]
             else:
                 total = sbuf([P, M], F32, "total%d" % c)[:]

@@ -26,7 +26,7 @@ TILES = H // P
 HALVES = S // BANK
 W1_LOADS = ((0, 1), (1, 2), (2, 3), (3, 4), (4, 6), (6, 8))
 EARLY_MIRROR = 5
-SQUARE_ON = "SSSSSVVV"
+SQUARE_ON = "SSGGGGGL"
 OWN_PAGES = 5
 
 
@@ -52,6 +52,11 @@ def tile_list_pressure_tap_survey_kernel(
         nc.vector.memset(tab_sc[:].bitcast(I32), 0)
         ident_f = sbuf([P, P], F32, "ident_f")
         make_identity(nc, ident_f[:])
+        for q in range(4):
+            nc.gpsimd.dma_start(
+                out=tab_sc[32 * q : 32 * q + 4 * K_PASSES, :].bitcast(I32),
+                in_=tab_scales[:, 4 * q : 4 * q + 4, :].bitcast(I32),
+            )
         vec_rows = sbuf([P, P], F32, "vec_rows")
         nc.vector.memset(vec_rows[32:64, :], 0.0)
         nc.vector.memset(vec_rows[64:128, :], 0.0)
@@ -94,14 +99,9 @@ def tile_list_pressure_tap_survey_kernel(
             pages[c] = sbuf([P, T2], F32, "page", tag=tag)
             nc.sync.dma_start(out=pages[c][:], in_=page0[P * c : P * (c + 1), :])
 
+        tabs = [load_table(0)]
         nc.sync.dma_start(idx[:], offs)
         nc.sync.dma_start(idx2[:], offs2)
-        tabs = [load_table(0)]
-        for q in range(4):
-            nc.sync.dma_start(
-                out=tab_sc[32 * q : 32 * q + 4 * K_PASSES, :].bitcast(I32),
-                in_=tab_scales[:, 4 * q : 4 * q + 4, :].bitcast(I32),
-            )
         tabs.append(load_table(1))
         load_w1(*W1_LOADS[0])
         for v, vec in enumerate((gain, reread, swing, mirror)):
@@ -143,25 +143,31 @@ def tile_list_pressure_tap_survey_kernel(
         grouped = {}
 
         def round_w1(c):
-            for a in range(K_PASSES):
-                g = sbuf([P, P, 4], BF16, "w1_grouped", tag="w1g%d_%d" % (a, c % 2))
+            first = sbuf([P, 2, P, 4], BF16, "w1_first", tag="w1_first%d" % (c % 2))
+            last = sbuf([P, P, 4], BF16, "w1_last", tag="w1g2_%d" % (c % 2))
+            for a, g in enumerate((first[:, 0], first[:, 1], last[:])):
                 nc.scalar.copy(
-                    g[:].rearrange("p (c j) i -> p c i j", j=4),
+                    g.rearrange("p (c j) i -> p c i j", j=4),
                     raws[c, a].rearrange("p i (c j) -> p c i j", j=4),
                 )
-                grouped[c, a] = g
+            grouped[c] = (first, last)
 
         w1q = {}
 
         def quantise_w1(c, tag):
-            codes = sbuf([P, K_PASSES, P], U32, "w1_codes", tag=tag)
-            scales = sbuf([P, K_PASSES, P], U8, "w1_scales%d" % c)
-            for a in ((0, 1, 2) if c < 2 else (2, 0, 1)):
-                nc.vector.quantize_mx(
-                    out=codes[:, a, :].bitcast(FP8X4),
-                    scales=scales[:, a, :],
-                    in_=grouped[c, a][:].rearrange("p c i -> p (c i)"),
-                )
+            codes = sbuf([P, K_PASSES * P], U32, "w1_codes", tag=tag)
+            scales = sbuf([P, K_PASSES * P], U8, "w1_scales%d" % c)
+            first, last = grouped[c]
+            nc.vector.quantize_mx(
+                out=codes[:, 2 * P : 3 * P].bitcast(FP8X4),
+                scales=scales[:, 2 * P : 3 * P],
+                in_=last[:].rearrange("p c i -> p (c i)"),
+            )
+            nc.vector.quantize_mx(
+                out=codes[:, 0 : 2 * P].bitcast(FP8X4),
+                scales=scales[:, 0 : 2 * P],
+                in_=first[:].rearrange("p a c i -> p (a c i)"),
+            )
             w1q[c] = (codes, scales)
 
         round_w1(0)
@@ -186,8 +192,8 @@ def tile_list_pressure_tap_survey_kernel(
             for a in range(K_PASSES):
                 nc.tensor.matmul_mx(
                     out=acc[:],
-                    lhsT=codes[:, a, :].bitcast(FP8X4),
-                    lhsT_scale=scales[:, a, :],
+                    lhsT=codes[:, P * a : P * (a + 1)].bitcast(FP8X4),
+                    lhsT_scale=scales[:, P * a : P * (a + 1)],
                     rhs=picked[a, h][:].bitcast(FP8X4),
                     rhs_scale=picked_sc[4 * a : P, BANK * h : BANK * (h + 1)],
                     start=(a == 0),
@@ -291,21 +297,24 @@ def tile_list_pressure_tap_survey_kernel(
         quantise_x(1, "x_codes1")
 
         early = sbuf([P, EARLY_MIRROR, M], F32, "early", tag="h%d" % ((TILES - 1) % 3))
-        late = sbuf([P, TILES - EARLY_MIRROR, M], F32, "late", tag="x_grouped")
-        held = sbuf([P, EARLY_MIRROR - 2, M], F32, "held", tag="x_t")
-        nc.scalar.activation(held[:, 0, 0:1], warm[:], ACT.Sqrt)
+        late = sbuf([P, TILES - EARLY_MIRROR + 1, M], F32, "late", tag="x_grouped")
+        warm_sqrt = sbuf([P, 1], F32, "warm_sqrt", tag="x_t")
+        nc.scalar.activation(warm_sqrt[:], warm[:], ACT.Sqrt)
 
         totals = []
+        after_y = []
         for c in range(TILES):
             taps4 = early[:, c, :] if c < EARLY_MIRROR else late[:, c - EARLY_MIRROR, :]
             nc.vector.tensor_copy(taps4, pages[c][:].indirect(idx4[:]))
             if c < 2:
                 total = sbuf([P, M], F32, "total", tag=("x_rows", "chain")[c])[:]
-            elif c < EARLY_MIRROR:
-                total = held[:, c - 2, :]
+            elif c == 4:
+                total = late[:, TILES - EARLY_MIRROR, :]
             else:
                 total = sbuf([P, M], F32, "total%d" % c)[:]
-            if SQUARE_ON[c] == "S":
+            if SQUARE_ON[c] == "L":
+                after_y.append((total, taps4))
+            elif SQUARE_ON[c] == "S":
                 nc.scalar.activation(total, taps4, ACT.Square)
             elif SQUARE_ON[c] == "V":
                 nc.vector.tensor_tensor(total, taps4, taps4, MULT)
@@ -335,9 +344,15 @@ def tile_list_pressure_tap_survey_kernel(
             sq = sbuf([P, M], F32, "y_sq", tag="raw%d_%d" % ((3, 4, 6)[c // 3], c % 3))
             nc.scalar.activation(sq[:], ys[c][:], ACT.Square)
             y_sq.append(sq)
+        for total, taps4 in after_y:
+            nc.scalar.activation(total, taps4, ACT.Square)
         for c in range(TILES):
-            nc.vector.scalar_tensor_tensor(
-                totals[c], totals[c], mirror_sq[:, c : c + 1], y_sq[c][:], MULT, ADD
-            )
-            nc.scalar.activation(totals[c], totals[c], ACT.Sqrt)
-            nc.sync.dma_start(out=out[P * c : P * (c + 1), :], in_=totals[c])
+            parts = 2 if c == TILES - 1 else 1
+            for part in range(parts):
+                ms = slice(M // parts * part, M // parts * (part + 1))
+                total = totals[c][:, ms]
+                nc.vector.scalar_tensor_tensor(
+                    total, total, mirror_sq[:, c : c + 1], y_sq[c][:, ms], MULT, ADD
+                )
+                nc.scalar.activation(total, total, ACT.Sqrt)
+                nc.sync.dma_start(out=out[P * c : P * (c + 1), ms], in_=total)

@@ -23,11 +23,15 @@ BANK = 512
 K_PASSES = K // 512
 R_PASSES = H // 512
 TILES = H // P
+LAST = TILES - 1
+TILES_PER_PASS = TILES // R_PASSES
 HALVES = S // BANK
+HALF_COLS = BANK // 16
+GAIN, REREAD, SWING, MIRROR = range(4)
 W1_LOADS = ((0, 1), (1, 2), (2, 3), (3, 4), (4, 6), (6, 8))
+OWN_PAGES = TILES - K_PASSES
 EARLY_MIRROR = 5
-SQUARE_ON = "SSGGGGGL"
-OWN_PAGES = 5
+SCALAR_SQUARES, GPSIMD_SQUARES = 3, 6
 
 
 def tile_list_pressure_tap_survey_kernel(
@@ -65,10 +69,10 @@ def tile_list_pressure_tap_survey_kernel(
         w4_sc = sbuf([P, R_PASSES, H], U8, "w4_sc")
         nc.vector.memset(w4_sc[:].rearrange("p a n -> p (a n)").bitcast(I32), 0)
 
-        warm = sbuf([P, 1], F32, "warm")
-        nc.vector.memset(warm[:], 1.0)
+        one = sbuf([P, 1], F32, "one")
+        nc.vector.memset(one[:], 1.0)
         warm_sin = sbuf([P, 1], F32, "warm_sin")
-        nc.scalar.activation(warm_sin[:], warm[:], ACT.Sin)
+        nc.scalar.activation(warm_sin[:], one[:], ACT.Sin)
 
         def load_table(a):
             words = sbuf([P, T], I32, "tab%d" % a)
@@ -77,7 +81,7 @@ def tile_list_pressure_tap_survey_kernel(
             )
             return words
 
-        raws = {}
+        w1_rows = {}
 
         def load_w1(first, last):
             for a in range(K_PASSES):
@@ -90,7 +94,7 @@ def tile_list_pressure_tap_survey_kernel(
                     ),
                 )
                 for c in range(first, last):
-                    raws[c, a] = raw[:, :, P * (c - first) : P * (c - first + 1)]
+                    w1_rows[c, a] = raw[:, :, P * (c - first) : P * (c - first + 1)]
 
         pages = {}
 
@@ -130,72 +134,73 @@ def tile_list_pressure_tap_survey_kernel(
                 in_=w4_scales[:, 4 * q : 4 * q + 4, :].rearrange("a r n -> r a n").bitcast(I32),
             )
 
-        vec_t = psum.tile([P, P], F32, name="vec_t", tag="t1", bufs=1)
+        vec_t = psum.tile([P, P], F32, name="vec_t", tag="turn", bufs=1)
         nc.tensor.transpose(vec_t[:], vec_rows[:], ident_f[:])
-        vecs = sbuf([P, 3 * TILES], F32, "vecs")
-        nc.scalar.copy(vecs[:], vec_t[:, 0 : 3 * TILES])
+        vecs = sbuf([P, MIRROR * TILES], F32, "vecs")
+        nc.scalar.copy(vecs[:], vec_t[:, 0 : MIRROR * TILES])
         mirror_sq = sbuf([P, TILES], F32, "mirror_sq")
-        nc.scalar.activation(mirror_sq[:], vec_t[:, 3 * TILES : 4 * TILES], ACT.Square)
+        nc.scalar.activation(
+            mirror_sq[:], vec_t[:, MIRROR * TILES : (MIRROR + 1) * TILES], ACT.Square
+        )
 
         def column(v, c):
             return vecs[:, TILES * v + c : TILES * v + c + 1]
 
-        grouped = {}
+        w1_bf16 = {}
 
         def round_w1(c):
-            first = sbuf([P, 2, P, 4], BF16, "w1_first", tag="w1_first%d" % (c % 2))
-            last = sbuf([P, P, 4], BF16, "w1_last", tag="w1g2_%d" % (c % 2))
-            for a, g in enumerate((first[:, 0], first[:, 1], last[:])):
+            passes01 = sbuf([P, 2, P, 4], BF16, "w1_passes01", tag="w1_passes01_%d" % (c % 2))
+            pass2 = sbuf([P, P, 4], BF16, "w1_pass2", tag="w1_pass2_%d" % (c % 2))
+            for a, rounded in enumerate((passes01[:, 0], passes01[:, 1], pass2[:])):
                 nc.scalar.copy(
-                    g.rearrange("p (c j) i -> p c i j", j=4),
-                    raws[c, a].rearrange("p i (c j) -> p c i j", j=4),
+                    rounded.rearrange("p (c j) i -> p c i j", j=4),
+                    w1_rows[c, a].rearrange("p i (c j) -> p c i j", j=4),
                 )
-            grouped[c] = (first, last)
+            w1_bf16[c] = (passes01, pass2)
 
-        w1q = {}
+        w1_mx = {}
 
-        def quantise_w1(c, tag):
-            codes = sbuf([P, K_PASSES * P], U32, "w1_codes", tag=tag)
+        def quantise_w1(c):
+            codes = sbuf([P, K_PASSES * P], U32, "w1_codes", tag="w1_codes%d" % (c % 2))
             scales = sbuf([P, K_PASSES * P], U8, "w1_scales%d" % c)
-            first, last = grouped[c]
+            passes01, pass2 = w1_bf16[c]
             nc.vector.quantize_mx(
                 out=codes[:, 2 * P : 3 * P].bitcast(FP8X4),
                 scales=scales[:, 2 * P : 3 * P],
-                in_=last[:].rearrange("p c i -> p (c i)"),
+                in_=pass2[:].rearrange("p c i -> p (c i)"),
             )
             nc.vector.quantize_mx(
                 out=codes[:, 0 : 2 * P].bitcast(FP8X4),
                 scales=scales[:, 0 : 2 * P],
-                in_=first[:].rearrange("p a c i -> p (a c i)"),
+                in_=passes01[:].rearrange("p a c i -> p (a c i)"),
             )
-            w1q[c] = (codes, scales)
+            w1_mx[c] = (codes, scales)
 
         round_w1(0)
-        quantise_w1(0, "w1_codes0")
+        quantise_w1(0)
 
         picked = {}
         picked_sc = sbuf([P, S], U8, "picked_sc")
         for a in range(K_PASSES):
-            for h in range(HALVES):
-                pk = sbuf([P, BANK], U32, "picked%d_%d" % (a, h))
-                nc.vector.tensor_copy(
-                    pk[:], tabs[a][:].bitcast(U32).indirect(idx[:, 32 * h : 32 * (h + 1)])
-                )
-                picked[a, h] = pk
+            for half in range(HALVES):
+                words = sbuf([P, BANK], U32, "picked%d_%d" % (a, half))
+                entries = idx[:, HALF_COLS * half : HALF_COLS * (half + 1)]
+                nc.vector.tensor_copy(words[:], tabs[a][:].bitcast(U32).indirect(entries))
+                picked[a, half] = words
             if a == 0:
                 nc.vector.tensor_copy(picked_sc[:], tab_sc[:].indirect(idx[:]))
             load_page(OWN_PAGES + a)
 
-        def first_product(c, h):
-            codes, scales = w1q[c]
-            acc = psum.tile([P, BANK], F32, name="acc", tag="acc", bufs=2)
+        def first_product(c, half):
+            codes, scales = w1_mx[c]
+            acc = psum.tile([P, BANK], F32, name="acc", tag="acc", bufs=HALVES)
             for a in range(K_PASSES):
                 nc.tensor.matmul_mx(
                     out=acc[:],
                     lhsT=codes[:, P * a : P * (a + 1)].bitcast(FP8X4),
                     lhsT_scale=scales[:, P * a : P * (a + 1)],
-                    rhs=picked[a, h][:].bitcast(FP8X4),
-                    rhs_scale=picked_sc[4 * a : P, BANK * h : BANK * (h + 1)],
+                    rhs=picked[a, half][:].bitcast(FP8X4),
+                    rhs_scale=picked_sc[4 * a : P, BANK * half : BANK * (half + 1)],
                     start=(a == 0),
                     stop=(a == K_PASSES - 1),
                 )
@@ -205,75 +210,72 @@ def tile_list_pressure_tap_survey_kernel(
 
         def make_h(c):
             magnitude = sbuf([P, S], F32, "magnitude", tag="chain")
-            h_tiles[c] = sbuf([P, S], F32, "h_tile", tag="h%d" % (c % 3))
-            for h in range(HALVES):
-                js = slice(BANK * h, BANK * (h + 1))
-                nc.scalar.activation(magnitude[:, js], first_product(c, h)[:], ACT.Abs)
+            h_tiles[c] = sbuf([P, S], F32, "h_tile", tag="h%d" % (c % 2))
+            for half in range(HALVES):
+                js = slice(BANK * half, BANK * (half + 1))
+                nc.scalar.activation(magnitude[:, js], first_product(c, half)[:], ACT.Abs)
                 nc.scalar.activation(
-                    h_tiles[c][:, js], magnitude[:, js], ACT.Copy, scale=column(0, c)
+                    h_tiles[c][:, js], magnitude[:, js], ACT.Copy, scale=column(GAIN, c)
                 )
 
-        x_t = {}
+        x_turned = {}
 
         def make_x(c):
-            taps = sbuf([P, M], F32, "taps", tag="w1g%d_%d" % (K_PASSES - 1, c % 2))
+            taps = sbuf([P, M], F32, "taps", tag="w1_pass2_%d" % (c % 2))
             nc.vector.tensor_copy(taps[:], pages[c][:].indirect(idx3[:]))
-            sine = sbuf([P, M], F32, "sine", tag="chain" if c < 7 else "x_rows")
-            nc.scalar.activation(sine[:], taps[:], ACT.Sin, scale=column(1, c))
-            x_rows = sbuf([P, M], BF16, "x_rows", tag="x_rows" if c < 7 else "chain")
-            nc.scalar.activation(x_rows[:], sine[:], ACT.Copy, scale=column(2, c))
-            turned = psum.tile([P, 4, P], BF16, name="turned", tag="t1", bufs=1)
-            for mb in range(4):
+            sine = sbuf([P, M], F32, "sine", tag="chain" if c < LAST else "x_rows")
+            nc.scalar.activation(sine[:], taps[:], ACT.Sin, scale=column(REREAD, c))
+            x_rows = sbuf([P, M], BF16, "x_rows", tag="x_rows" if c < LAST else "chain")
+            nc.scalar.activation(x_rows[:], sine[:], ACT.Copy, scale=column(SWING, c))
+            turned = psum.tile([P, M // P, P], BF16, name="turned", tag="turn", bufs=1)
+            for mb in range(M // P):
                 nc.tensor.transpose(turned[:, mb, :], x_rows[:, P * mb : P * (mb + 1)], ident_b[:])
-            b, cc = divmod(c, 4)
-            if cc == 0:
-                x_t[b] = sbuf([P, 4, 2, P], F32, "x_t", tag="x_t")
+            b, quarter = divmod(c, TILES_PER_PASS)
+            if quarter == 0:
+                x_turned[b] = sbuf([P, M // P, 2, P], F32, "x_turned")
             nc.scalar.copy(
-                x_t[b][:, :, :, 32 * cc : 32 * (cc + 1)],
-                turned[:].bitcast(F32).rearrange("m b (p u) -> m b u p", u=2),
+                x_turned[b][:, :, :, 32 * quarter : 32 * (quarter + 1)],
+                turned[:].bitcast(F32).rearrange("m mb (p u) -> m mb u p", u=2),
             )
 
-        x_grouped = {}
+        x_mx = {}
 
-        def deal_x(b):
-            xg = sbuf([P, M, 2], F32, "x_grouped", tag="x_grouped")
-            for hb in range(2):
-                back = psum.tile([P, 2, 2, P], F32, name="back", tag="t2", bufs=2)
+        def quantise_x(b):
+            x_words = sbuf([P, M, 2], F32, "x_words")
+            for pair in range(2):
+                back = psum.tile([P, 2, 2, P], F32, name="back", tag="back", bufs=2)
                 for mb in range(2):
                     for u in range(2):
                         nc.tensor.transpose(
-                            back[:, mb, u, :], x_t[b][:, 2 * hb + mb, u, :], ident_f[:]
+                            back[:, mb, u, :], x_turned[b][:, 2 * pair + mb, u, :], ident_f[:]
                         )
                 nc.scalar.copy(
-                    xg[:, 256 * hb : 256 * (hb + 1), :].rearrange("p (b m) u -> p b m u", b=2),
-                    back[:].rearrange("p b u m -> p b m u"),
+                    x_words[:, 2 * P * pair : 2 * P * (pair + 1), :].rearrange(
+                        "p (mb m) u -> p mb m u", mb=2
+                    ),
+                    back[:].rearrange("p mb u m -> p mb m u"),
                 )
-            x_grouped[b] = xg
-
-        xq = {}
-
-        def quantise_x(b, tag):
-            codes = sbuf([P, M], U32, "x_codes", tag=tag)
+            codes = sbuf([P, M], U32, "x_codes%d" % b)
             scales = sbuf([P, M], U8, "x_scales%d" % b)
             nc.vector.quantize_mx(
                 out=codes[:].bitcast(FP8X4),
                 scales=scales[:],
-                in_=x_grouped[b][:].rearrange("p m u -> p (m u)").bitcast(BF16),
+                in_=x_words[:].rearrange("p m u -> p (m u)").bitcast(BF16),
             )
-            xq[b] = (codes, scales)
+            x_mx[b] = (codes, scales)
 
-        h_tiles[0] = sbuf([P, S], F32, "h_tile", tag="h0")
-        for h in range(HALVES):
-            js = slice(BANK * h, BANK * (h + 1))
-            if h == 1:
+        magnitude0 = sbuf([P, S], F32, "magnitude0", tag="h0")
+        for half in range(HALVES):
+            js = slice(BANK * half, BANK * (half + 1))
+            if half == 1:
                 round_w1(1)
-                quantise_w1(1, "w1_codes1")
-            gained = sbuf([P, BANK], F32, "gained", tag="raw%d_%d" % (h, K_PASSES - 1))
-            nc.scalar.activation(gained[:], wgs_sb[:, js], ACT.Copy, scale=column(0, 0))
-            nc.scalar.activation(h_tiles[0][:, js], first_product(0, h)[:], ACT.Abs)
+                quantise_w1(1)
+            gained = sbuf([P, BANK], F32, "gained", tag="raw%d_%d" % (half, K_PASSES - 1))
+            nc.scalar.activation(gained[:], wgs_sb[:, js], ACT.Copy, scale=column(GAIN, 0))
+            nc.scalar.activation(magnitude0[:, js], first_product(0, half)[:], ACT.Abs)
             nc.vector.tensor_tensor(
-                pages[0][:].indirect(idx2[:, 32 * h : 32 * (h + 1)]),
-                h_tiles[0][:, js], gained[:], MULT,
+                pages[0][:].indirect(idx2[:, HALF_COLS * half : HALF_COLS * (half + 1)]),
+                magnitude0[:, js], gained[:], MULT,
             )
 
         for c in range(TILES):
@@ -281,54 +283,48 @@ def tile_list_pressure_tap_survey_kernel(
                 round_w1(c + 2)
             if c + 1 < TILES:
                 make_h(c + 1)
-            if c == 4:
-                deal_x(0)
+            if c == TILES_PER_PASS:
+                quantise_x(0)
             if c > 0:
                 nc.vector.tensor_tensor(
                     pages[c][:].indirect(idx2[:]), h_tiles[c][:], wgs_sb[:], MULT
                 )
             if c + 2 < TILES:
-                quantise_w1(c + 2, "h%d" % (c % 3))
-            if c == 6:
-                quantise_x(0, "h%d" % (c % 3))
+                quantise_w1(c + 2)
             make_x(c)
 
-        deal_x(1)
-        quantise_x(1, "x_codes1")
+        quantise_x(1)
 
-        early = sbuf([P, EARLY_MIRROR, M], F32, "early", tag="h%d" % ((TILES - 1) % 3))
-        late = sbuf([P, TILES - EARLY_MIRROR + 1, M], F32, "late", tag="x_grouped")
-        warm_sqrt = sbuf([P, 1], F32, "warm_sqrt", tag="x_t")
-        nc.scalar.activation(warm_sqrt[:], warm[:], ACT.Sqrt)
+        early = sbuf([P, EARLY_MIRROR - 1, M], F32, "early", tag="h%d" % (LAST % 2))
+        early_one = sbuf([P, M], F32, "early_one", tag="wgs_sb")
+        mirrored = [early[:, c, :] for c in range(EARLY_MIRROR - 1)]
+        mirrored.insert(SCALAR_SQUARES - 1, early_one[:])
+        for c in range(EARLY_MIRROR):
+            nc.vector.tensor_copy(mirrored[c], pages[c][:].indirect(idx4[:]))
 
         totals = []
-        after_y = []
-        for c in range(TILES):
-            taps4 = early[:, c, :] if c < EARLY_MIRROR else late[:, c - EARLY_MIRROR, :]
-            nc.vector.tensor_copy(taps4, pages[c][:].indirect(idx4[:]))
-            if c < 2:
-                total = sbuf([P, M], F32, "total", tag=("x_rows", "chain")[c])[:]
-            elif c == 4:
-                total = late[:, TILES - EARLY_MIRROR, :]
-            else:
-                total = sbuf([P, M], F32, "total%d" % c)[:]
-            if SQUARE_ON[c] == "L":
-                after_y.append((total, taps4))
-            elif SQUARE_ON[c] == "S":
-                nc.scalar.activation(total, taps4, ACT.Square)
-            elif SQUARE_ON[c] == "V":
-                nc.vector.tensor_tensor(total, taps4, taps4, MULT)
-            else:
-                nc.gpsimd.tensor_tensor(total, taps4, taps4, MULT)
-            totals.append(total)
+        for c, tag in enumerate(("x_rows", "chain", "x_turned")):
+            total = sbuf([P, M + 1], F32, "total", tag=tag)
+            nc.scalar.activation(total[:, 0:M], mirrored[c], ACT.Square)
+            totals.append(total[:, 0:M])
+        nc.scalar.activation(total[:, M : M + 1], one[:], ACT.Sqrt)
 
-        y_tags = [("y", 3)] * 3 + [("acc", 2)] * 2 + [("t2", 2)] * 2 + [("t1", 1)]
-        ys = []
-        for c in range(TILES):
-            tag, bufs = y_tags[c]
-            ys.append(psum.tile([P, M], F32, name="y", tag=tag, bufs=bufs))
+        late = sbuf([P, TILES - EARLY_MIRROR, M], F32, "late", tag="wgs_sb")
+        for c in range(EARLY_MIRROR, TILES):
+            mirrored.append(late[:, c - EARLY_MIRROR, :])
+            nc.vector.tensor_copy(mirrored[c], pages[c][:].indirect(idx4[:]))
+        pooled = sbuf([P, GPSIMD_SQUARES - SCALAR_SQUARES, M], F32, "pooled", tag="x_words")
+        for c in range(SCALAR_SQUARES, GPSIMD_SQUARES):
+            totals.append(pooled[:, c - SCALAR_SQUARES, :])
+            nc.gpsimd.tensor_tensor(totals[c], mirrored[c], mirrored[c], MULT)
+        for c in range(GPSIMD_SQUARES, TILES):
+            totals.append(sbuf([P, M], F32, "total%d" % c)[:])
+            nc.vector.tensor_tensor(totals[c], mirrored[c], mirrored[c], MULT)
+
+        y_banks = [("y", 3)] * 3 + [("acc", HALVES)] * HALVES + [("back", 2)] * 2 + [("turn", 1)]
+        ys = [psum.tile([P, M], F32, name="y", tag=tag, bufs=bufs) for tag, bufs in y_banks]
         for b in range(R_PASSES):
-            codes, scales = xq[b]
+            codes, scales = x_mx[b]
             for c in range(TILES):
                 nc.tensor.matmul_mx(
                     out=ys[c][:],
@@ -339,15 +335,13 @@ def tile_list_pressure_tap_survey_kernel(
                     start=(b == 0),
                     stop=(b == R_PASSES - 1),
                 )
+        spare = ["raw%d_%d" % (first, a) for first, last in W1_LOADS[3:] for a in range(K_PASSES)]
         y_sq = []
         for c in range(TILES):
-            sq = sbuf([P, M], F32, "y_sq", tag="raw%d_%d" % ((3, 4, 6)[c // 3], c % 3))
-            nc.scalar.activation(sq[:], ys[c][:], ACT.Square)
-            y_sq.append(sq)
-        for total, taps4 in after_y:
-            nc.scalar.activation(total, taps4, ACT.Square)
+            y_sq.append(sbuf([P, M], F32, "y_sq", tag=spare[c]))
+            nc.scalar.activation(y_sq[c][:], ys[c][:], ACT.Square)
         for c in range(TILES):
-            parts = 2 if c == TILES - 1 else 1
+            parts = 2 if c == LAST else 1
             for part in range(parts):
                 ms = slice(M // parts * part, M // parts * (part + 1))
                 total = totals[c][:, ms]

from contextlib import ExitStack

import concourse.mybir as mybir
from concourse.masks import make_identity

F32 = mybir.dt.float32
BF16 = mybir.dt.bfloat16
I32 = mybir.dt.int32
U32 = mybir.dt.uint32
U16 = mybir.dt.uint16
U8 = mybir.dt.uint8
FP8X4 = mybir.dt.float8_e4m3fn_x4
FP4X4 = mybir.dt.float4_e2m1fn_x4
ACT = mybir.ActivationFunctionType
MULT = mybir.AluOpType.mult
ADD = mybir.AluOpType.add

K, H, T, S, T2, M = 1536, 1024, 4096, 1024, 2048, 512
FLOPS = 2 * K * H * S + 2 * H * H * M

P = 128
BANK = 512
K_PASSES = K // 512
R_PASSES = H // 512
TILES = H // P
LAST = TILES - 1
TILES_PER_PASS = TILES // R_PASSES
HALVES = S // BANK
HALF_COLS = BANK // 16
GAIN, REREAD, SWING, MIRROR = range(4)
W1_LOADS = ((0, 1), (1, 2), (2, 3), (3, 4), (4, 6), (6, 8))
OWN_PAGES = TILES - K_PASSES
EARLY_MIRROR = 5
SCALAR_SQUARES, GPSIMD_SQUARES = 3, 6


def tile_list_pressure_tap_survey_kernel(
    tc, tab_words, tab_scales, offs, offs2, offs3, offs4, w1, gain, wgs, page0,
    reread, swing, w4_words, w4_scales, mirror, out,
):
    nc = tc.nc
    with ExitStack() as ctx:
        lists = ctx.enter_context(tc.tile_pool(name="lists", bufs=1))
        sb = ctx.enter_context(tc.tile_pool(name="sb", bufs=1))
        psum = ctx.enter_context(tc.psum_pool(name="psum", bufs=1))

        def sbuf(shape, dtype, name, tag=None):
            return sb.tile(shape, dtype, name=name, tag=tag or name, align_bytes=64)

        idx = lists.tile([P, S // 16], U16, name="idx")
        idx2 = lists.tile([P, S // 16], U16, name="idx2")
        idx3 = lists.tile([P, M // 16], U16, name="idx3")
        idx4 = lists.tile([P, M // 16], U16, name="idx4")

        tab_sc = sbuf([P, T], U8, "tab_sc")
        nc.vector.memset(tab_sc[:].bitcast(I32), 0)
        ident_f = sbuf([P, P], F32, "ident_f")
        make_identity(nc, ident_f[:])
        for q in range(4):
            nc.gpsimd.dma_start(
                out=tab_sc[32 * q : 32 * q + 4 * K_PASSES, :].bitcast(I32),
                in_=tab_scales[:, 4 * q : 4 * q + 4, :].bitcast(I32),
            )
        vec_rows = sbuf([P, P], F32, "vec_rows")
        nc.vector.memset(vec_rows[32:64, :], 0.0)
        nc.vector.memset(vec_rows[64:128, :], 0.0)
        ident_b = sbuf([P, P], BF16, "ident_b")
        nc.vector.tensor_copy(ident_b[:], ident_f[:])
        w4_sc = sbuf([P, R_PASSES, H], U8, "w4_sc")
        nc.vector.memset(w4_sc[:].rearrange("p a n -> p (a n)").bitcast(I32), 0)

        one = sbuf([P, 1], F32, "one")
        nc.vector.memset(one[:], 1.0)
        warm_sin = sbuf([P, 1], F32, "warm_sin")
        nc.scalar.activation(warm_sin[:], one[:], ACT.Sin)

        def load_table(a):
            words = sbuf([P, T], I32, "tab%d" % a)
            nc.sync.dma_start(
                out=words[:], in_=tab_words[a].rearrange("p n i -> p (n i)").bitcast(I32)
            )
            return words

        w1_rows = {}

        def load_w1(first, last):
            for a in range(K_PASSES):
                tag = "chain" if (first, a) == (2, K_PASSES - 1) else "raw%d_%d" % (first, a)
                raw = sbuf([P, 4, P * (last - first)], F32, "raw", tag=tag)
                nc.sync.dma_start(
                    out=raw[:],
                    in_=w1[512 * a : 512 * (a + 1), P * first : P * last].rearrange(
                        "(p i) c -> p i c", i=4
                    ),
                )
                for c in range(first, last):
                    w1_rows[c, a] = raw[:, :, P * (c - first) : P * (c - first + 1)]

        pages = {}

        def load_page(c):
            tag = "page%d" % c if c < OWN_PAGES else "tab%d" % (c - OWN_PAGES)
            pages[c] = sbuf([P, T2], F32, "page", tag=tag)
            nc.sync.dma_start(out=pages[c][:], in_=page0[P * c : P * (c + 1), :])

        tabs = [load_table(0)]
        nc.sync.dma_start(idx[:], offs)
        nc.sync.dma_start(idx2[:], offs2)
        tabs.append(load_table(1))
        load_w1(*W1_LOADS[0])
        for v, vec in enumerate((gain, reread, swing, mirror)):
            nc.sync.dma_start(
                out=vec_rows[TILES * v : TILES * (v + 1), :],
                in_=vec.rearrange("(c p) -> c p", p=P),
            )
        tabs.append(load_table(2))
        wgs_sb = sbuf([P, S], F32, "wgs_sb")
        nc.sync.dma_start(out=wgs_sb[:, 0:BANK], in_=wgs[:, 0:BANK])
        load_page(0)
        load_w1(*W1_LOADS[1])
        nc.sync.dma_start(out=wgs_sb[:, BANK:S], in_=wgs[:, BANK:S])
        nc.sync.dma_start(idx3[:], offs3)
        for n, (first, last) in enumerate(W1_LOADS[2:]):
            load_w1(first, last)
            load_page(n + 1)
        nc.sync.dma_start(idx4[:], offs4)
        w4 = sbuf([P, R_PASSES, 2 * H], U8, "w4")
        nc.sync.dma_start(
            out=w4[:].bitcast(I32), in_=w4_words.rearrange("a p n -> p a n").bitcast(I32)
        )
        for q in range(4):
            nc.sync.dma_start(
                out=w4_sc[32 * q : 32 * q + 4, :, :].bitcast(I32),
                in_=w4_scales[:, 4 * q : 4 * q + 4, :].rearrange("a r n -> r a n").bitcast(I32),
            )

        vec_t = psum.tile([P, P], F32, name="vec_t", tag="turn", bufs=1)
        nc.tensor.transpose(vec_t[:], vec_rows[:], ident_f[:])
        vecs = sbuf([P, MIRROR * TILES], F32, "vecs")
        nc.scalar.copy(vecs[:], vec_t[:, 0 : MIRROR * TILES])
        mirror_sq = sbuf([P, TILES], F32, "mirror_sq")
        nc.scalar.activation(
            mirror_sq[:], vec_t[:, MIRROR * TILES : (MIRROR + 1) * TILES], ACT.Square
        )

        def column(v, c):
            return vecs[:, TILES * v + c : TILES * v + c + 1]

        w1_bf16 = {}

        def round_w1(c):
            passes01 = sbuf([P, 2, P, 4], BF16, "w1_passes01", tag="w1_passes01_%d" % (c % 2))
            pass2 = sbuf([P, P, 4], BF16, "w1_pass2", tag="w1_pass2_%d" % (c % 2))
            for a, rounded in enumerate((passes01[:, 0], passes01[:, 1], pass2[:])):
                nc.scalar.copy(
                    rounded.rearrange("p (c j) i -> p c i j", j=4),
                    w1_rows[c, a].rearrange("p i (c j) -> p c i j", j=4),
                )
            w1_bf16[c] = (passes01, pass2)

        w1_mx = {}

        def quantise_w1(c):
            codes = sbuf([P, K_PASSES * P], U32, "w1_codes", tag="w1_codes%d" % (c % 2))
            scales = sbuf([P, K_PASSES * P], U8, "w1_scales%d" % c)
            passes01, pass2 = w1_bf16[c]
            nc.vector.quantize_mx(
                out=codes[:, 2 * P : 3 * P].bitcast(FP8X4),
                scales=scales[:, 2 * P : 3 * P],
                in_=pass2[:].rearrange("p c i -> p (c i)"),
            )
            nc.vector.quantize_mx(
                out=codes[:, 0 : 2 * P].bitcast(FP8X4),
                scales=scales[:, 0 : 2 * P],
                in_=passes01[:].rearrange("p a c i -> p (a c i)"),
            )
            w1_mx[c] = (codes, scales)

        round_w1(0)
        quantise_w1(0)

        picked = {}
        picked_sc = sbuf([P, S], U8, "picked_sc")
        for a in range(K_PASSES):
            for half in range(HALVES):
                words = sbuf([P, BANK], U32, "picked%d_%d" % (a, half))
                entries = idx[:, HALF_COLS * half : HALF_COLS * (half + 1)]
                nc.vector.tensor_copy(words[:], tabs[a][:].bitcast(U32).indirect(entries))
                picked[a, half] = words
            if a == 0:
                nc.vector.tensor_copy(picked_sc[:], tab_sc[:].indirect(idx[:]))
            load_page(OWN_PAGES + a)

        def first_product(c, half):
            codes, scales = w1_mx[c]
            acc = psum.tile([P, BANK], F32, name="acc", tag="acc", bufs=HALVES)
            for a in range(K_PASSES):
                nc.tensor.matmul_mx(
                    out=acc[:],
                    lhsT=codes[:, P * a : P * (a + 1)].bitcast(FP8X4),
                    lhsT_scale=scales[:, P * a : P * (a + 1)],
                    rhs=picked[a, half][:].bitcast(FP8X4),
                    rhs_scale=picked_sc[4 * a : P, BANK * half : BANK * (half + 1)],
                    start=(a == 0),
                    stop=(a == K_PASSES - 1),
                )
            return acc

        h_tiles = {}

        def make_h(c):
            magnitude = sbuf([P, S], F32, "magnitude", tag="chain")
            h_tiles[c] = sbuf([P, S], F32, "h_tile", tag="h%d" % (c % 2))
            for half in range(HALVES):
                js = slice(BANK * half, BANK * (half + 1))
                nc.scalar.activation(magnitude[:, js], first_product(c, half)[:], ACT.Abs)
                nc.scalar.activation(
                    h_tiles[c][:, js], magnitude[:, js], ACT.Copy, scale=column(GAIN, c)
                )

        x_turned = {}

        def make_x(c):
            taps = sbuf([P, M], F32, "taps", tag="w1_pass2_%d" % (c % 2))
            nc.vector.tensor_copy(taps[:], pages[c][:].indirect(idx3[:]))
            sine = sbuf([P, M], F32, "sine", tag="chain" if c < LAST else "x_rows")
            nc.scalar.activation(sine[:], taps[:], ACT.Sin, scale=column(REREAD, c))
            x_rows = sbuf([P, M], BF16, "x_rows", tag="x_rows" if c < LAST else "chain")
            nc.scalar.activation(x_rows[:], sine[:], ACT.Copy, scale=column(SWING, c))
            turned = psum.tile([P, M // P, P], BF16, name="turned", tag="turn", bufs=1)
            for mb in range(M // P):
                nc.tensor.transpose(turned[:, mb, :], x_rows[:, P * mb : P * (mb + 1)], ident_b[:])
            b, quarter = divmod(c, TILES_PER_PASS)
            if quarter == 0:
                x_turned[b] = sbuf([P, M // P, 2, P], F32, "x_turned")
            nc.scalar.copy(
                x_turned[b][:, :, :, 32 * quarter : 32 * (quarter + 1)],
                turned[:].bitcast(F32).rearrange("m mb (p u) -> m mb u p", u=2),
            )

        x_mx = {}

        def quantise_x(b):
            x_words = sbuf([P, M, 2], F32, "x_words")
            for pair in range(2):
                back = psum.tile([P, 2, 2, P], F32, name="back", tag="back", bufs=2)
                for mb in range(2):
                    for u in range(2):
                        nc.tensor.transpose(
                            back[:, mb, u, :], x_turned[b][:, 2 * pair + mb, u, :], ident_f[:]
                        )
                nc.scalar.copy(
                    x_words[:, 2 * P * pair : 2 * P * (pair + 1), :].rearrange(
                        "p (mb m) u -> p mb m u", mb=2
                    ),
                    back[:].rearrange("p mb u m -> p mb m u"),
                )
            codes = sbuf([P, M], U32, "x_codes%d" % b)
            scales = sbuf([P, M], U8, "x_scales%d" % b)
            nc.vector.quantize_mx(
                out=codes[:].bitcast(FP8X4),
                scales=scales[:],
                in_=x_words[:].rearrange("p m u -> p (m u)").bitcast(BF16),
            )
            x_mx[b] = (codes, scales)

        magnitude0 = sbuf([P, S], F32, "magnitude0", tag="h0")
        for half in range(HALVES):
            js = slice(BANK * half, BANK * (half + 1))
            if half == 1:
                round_w1(1)
                quantise_w1(1)
            gained = sbuf([P, BANK], F32, "gained", tag="raw%d_%d" % (half, K_PASSES - 1))
            nc.scalar.activation(gained[:], wgs_sb[:, js], ACT.Copy, scale=column(GAIN, 0))
            nc.scalar.activation(magnitude0[:, js], first_product(0, half)[:], ACT.Abs)
            nc.vector.tensor_tensor(
                pages[0][:].indirect(idx2[:, HALF_COLS * half : HALF_COLS * (half + 1)]),
                magnitude0[:, js], gained[:], MULT,
            )

        for c in range(TILES):
            if c + 2 < TILES:
                round_w1(c + 2)
            if c + 1 < TILES:
                make_h(c + 1)
            if c == TILES_PER_PASS:
                quantise_x(0)
            if c > 0:
                nc.vector.tensor_tensor(
                    pages[c][:].indirect(idx2[:]), h_tiles[c][:], wgs_sb[:], MULT
                )
            if c + 2 < TILES:
                quantise_w1(c + 2)
            make_x(c)

        quantise_x(1)

        early = sbuf([P, EARLY_MIRROR - 1, M], F32, "early", tag="h%d" % (LAST % 2))
        early_one = sbuf([P, M], F32, "early_one", tag="wgs_sb")
        mirrored = [early[:, c, :] for c in range(EARLY_MIRROR - 1)]
        mirrored.insert(SCALAR_SQUARES - 1, early_one[:])
        for c in range(EARLY_MIRROR):
            nc.vector.tensor_copy(mirrored[c], pages[c][:].indirect(idx4[:]))

        totals = []
        for c, tag in enumerate(("x_rows", "chain", "x_turned")):
            total = sbuf([P, M + 1], F32, "total", tag=tag)
            nc.scalar.activation(total[:, 0:M], mirrored[c], ACT.Square)
            totals.append(total[:, 0:M])
        nc.scalar.activation(total[:, M : M + 1], one[:], ACT.Sqrt)

        late = sbuf([P, TILES - EARLY_MIRROR, M], F32, "late", tag="wgs_sb")
        for c in range(EARLY_MIRROR, TILES):
            mirrored.append(late[:, c - EARLY_MIRROR, :])
            nc.vector.tensor_copy(mirrored[c], pages[c][:].indirect(idx4[:]))
        pooled = sbuf([P, GPSIMD_SQUARES - SCALAR_SQUARES, M], F32, "pooled", tag="x_words")
        for c in range(SCALAR_SQUARES, GPSIMD_SQUARES):
            totals.append(pooled[:, c - SCALAR_SQUARES, :])
            nc.gpsimd.tensor_tensor(totals[c], mirrored[c], mirrored[c], MULT)
        for c in range(GPSIMD_SQUARES, TILES):
            totals.append(sbuf([P, M], F32, "total%d" % c)[:])
            nc.vector.tensor_tensor(totals[c], mirrored[c], mirrored[c], MULT)

        y_banks = [("y", 3)] * 3 + [("acc", HALVES)] * HALVES + [("back", 2)] * 2 + [("turn", 1)]
        ys = [psum.tile([P, M], F32, name="y", tag=tag, bufs=bufs) for tag, bufs in y_banks]
        for b in range(R_PASSES):
            codes, scales = x_mx[b]
            for c in range(TILES):
                nc.tensor.matmul_mx(
                    out=ys[c][:],
                    lhsT=w4[:, b, 2 * P * c : 2 * P * (c + 1)].bitcast(FP4X4),
                    lhsT_scale=w4_sc[:, b, P * c : P * (c + 1)],
                    rhs=codes[:].bitcast(FP8X4),
                    rhs_scale=scales[:],
                    start=(b == 0),
                    stop=(b == R_PASSES - 1),
                )
        spare = ["raw%d_%d" % (first, a) for first, last in W1_LOADS[3:] for a in range(K_PASSES)]
        y_sq = []
        for c in range(TILES):
            y_sq.append(sbuf([P, M], F32, "y_sq", tag=spare[c]))
            nc.scalar.activation(y_sq[c][:], ys[c][:], ACT.Square)
        for c in range(TILES):
            parts = 2 if c == LAST else 1
            for part in range(parts):
                ms = slice(M // parts * part, M // parts * (part + 1))
                total = totals[c][:, ms]
                nc.vector.scalar_tensor_tensor(
                    total, total, mirror_sq[:, c : c + 1], y_sq[c][:, ms], MULT, ADD
                )
                nc.scalar.activation(total, total, ACT.Sqrt)
                nc.sync.dma_start(out=out[P * c : P * (c + 1), ms], in_=total)
